import numpy as np
import ml_dtypes


def mxq(x, axis, fmt="e4m3"):
    dtype, down = {"e4m3": (ml_dtypes.float8_e4m3fn, 7), "e5m2": (ml_dtypes.float8_e5m2, 14)}[fmt]
    v = np.moveaxis(np.asarray(x, np.float32).astype(ml_dtypes.bfloat16).astype(np.float64), axis, -1)
    blocks = v.reshape(v.shape[:-1] + (-1, 32))
    amax = np.abs(blocks).max(-1, keepdims=True)
    byte = np.maximum(np.where(amax > 0, np.frexp(amax)[1] - 1 + 127, 0) - down, 1)
    scale = np.exp2(byte - 127.0)
    codes = (blocks / scale).astype(np.float32).astype(dtype).astype(np.float64)
    return np.moveaxis((codes * scale).reshape(v.shape), -1, axis)


WIDE = False


def mx_kscale(k):
    if not WIDE:
        return np.ones(k)
    levels = np.array([10, -10, 5, -5, 0])
    if k % 512:
        return np.exp2(np.random.permutation(np.resize(levels, k // 32))).repeat(32)
    a = np.empty((k // 512, 16))
    for p in range(k // 512):
        a[p, :8] = np.random.permutation(np.resize(levels, 8))
        for g in range(8):
            far = levels[np.abs(levels - a[p, g]) >= 10]
            a[p, g + 8] = far[np.random.randint(len(far))]
    return np.exp2(a.ravel()).repeat(32)


def f64(x):
    return np.asarray(x).astype(np.float64)


def striped(idx):
    return np.tile(idx.reshape(-1, 16).T, (8, 1)).astype(np.uint16)


def unstriped(offs):
    return offs[:16].T.reshape(-1).astype(np.int64)


def striped8(idx):
    return np.concatenate([x.reshape(-1, 16).T for x in idx]).astype(np.uint16)


def runs(offs, k):
    lists = np.stack([offs[16 * r : 16 * r + 16].T.reshape(-1) for r in range(8)]).astype(np.int64)
    return lists[np.arange(k) % 512 // 64]


def pack_weight(w):
    k, n = w.shape
    w = f64(np.asarray(w, np.float32).astype(ml_dtypes.bfloat16)).reshape(k // 32, 32, n)
    amax = np.abs(w).max(1)
    byte = np.clip(np.where(amax > 0, np.frexp(amax)[1] - 1 + 127 - 7, 1), 1, 254)
    scaled = (w * np.exp2(127.0 - byte)[:, None, :]).reshape(k, n).astype(np.float32)
    words = np.ascontiguousarray(scaled.reshape(k // 512, 128, 4, n).transpose(0, 1, 3, 2)).astype(ml_dtypes.float8_e4m3fn).view(np.uint8)
    return words, np.ascontiguousarray(byte.astype(np.uint8).reshape(k // 512, 16, n))


def unpack_weight(words, scales):
    g, p, n, _ = words.shape
    vals = np.ascontiguousarray(words).view(ml_dtypes.float8_e4m3fn).astype(np.float64) * np.repeat(np.exp2(scales.astype(np.float64) - 127.0), 8, axis=1)[..., None]
    return vals.transpose(0, 1, 3, 2).reshape(g * 512, n)

def planes(y):
    n, m = y.shape
    v = y.astype(np.float32).astype(ml_dtypes.bfloat16).astype(np.float64).reshape(n // 32, 32, m)
    top = np.abs(v).max(1)
    byte = np.clip(np.where(top > 0, np.frexp(top)[1] - 1 + 127 - 7, 1), 1, 254)
    codes = (v * np.exp2(127.0 - byte)[:, None, :]).reshape(n, m).astype(np.float32).astype(ml_dtypes.float8_e4m3fn).view(np.uint8)
    words = codes.reshape(n // 512, 128, 4, m).transpose(0, 1, 3, 2)
    return np.ascontiguousarray(words), np.ascontiguousarray(byte.astype(np.uint8).reshape(n // 512, 16, m))


K, T, S, G, H, W, U = 512, 2048, 512, 2048, 512, 256, 1024


def setup_inputs():
    n = np.random.standard_normal
    s = mx_kscale(K)[:, None]
    packed_xT = pack_weight(n((K, T)) * s)
    packed_dT = pack_weight(n((K, G)) / s)
    perm = np.stack([np.random.permutation(S) for _ in range(8)])
    return {
        "x_words": packed_xT[0],
        "x_scales": packed_xT[1],
        "d_words": packed_dT[0],
        "d_scales": packed_dT[1],
        "gs": (np.random.uniform(0.5, 1.5, (K, 1)) * s).astype(np.float32),
        "mem": n((H, U)).astype(np.float32),
        "offs": striped(np.random.permutation(T)[:S]),
        "ci": striped(np.random.permutation(G)[:H]),
        "n1": striped8(perm[:, :W]),
        "n2": striped8(perm[:, W:]),
        "n3": striped8(np.stack([np.random.permutation(S) for _ in range(8)])),
        "k1": striped8(np.random.randint(0, G, (8, H))),
        "n4": striped8(np.stack([np.random.permutation(U)[:S] for _ in range(8)])),
    }


def reference(x_words, x_scales, d_words, d_scales, gs, mem, offs, ci, n1, n2, n3, k1, n4):
    d_k1 = unpack_weight(d_words, d_scales)[np.arange(K)[:, None], runs(k1, K)]
    d_ci = unpack_weight(d_words, d_scales)[:, unstriped(ci)]
    xq = unpack_weight(x_words, x_scales)[:, unstriped(offs)]
    s = 0.0625 * (d_ci.T @ xq)
    pa = s[np.arange(H)[:, None], runs(n1, H)]
    pb = s[np.arange(H)[:, None], runs(n2, H)]
    rb = pa - pb
    ra = pa + pb
    ds = np.zeros((H, S))
    ds[np.arange(H)[:, None], runs(n1, H)] = ra
    dt = ds.copy()
    dt[np.arange(H)[:, None], runs(n2, H)] = rb
    z = f64(gs) * (np.maximum(dt, dt[np.arange(H)[:, None], runs(n3, H)]))
    h = 0.0625 * ((d_k1.T @ mxq(z, 0, "e4m3")))
    nw = np.maximum(h, 0.5 * (f64(mem)[np.arange(H)[:, None], runs(n4, H)]))
    out = f64(mem).copy()
    out[np.arange(H)[:, None], runs(n4, H)] = nw
    return (out,) + planes(out)

from contextlib import ExitStack

import concourse.mybir as mybir

K, T, S, G, H, W, U = 512, 2048, 512, 2048, 512, 256, 1024
FLOPS = 2 * K * H * S + 2 * H * H * S

F32 = mybir.dt.float32
BF16 = mybir.dt.bfloat16
I32 = mybir.dt.int32
U32 = mybir.dt.uint32
U16 = mybir.dt.uint16
U8 = mybir.dt.uint8
FP8X4 = mybir.dt.float8_e4m3fn_x4
ADD = mybir.AluOpType.add
MULT = mybir.AluOpType.mult
MAX = mybir.AluOpType.max
COPY = mybir.ActivationFunctionType.Copy

P = 128
PACK = 4
HALF = S // 2
QUARTER = U // 4


def tile_picked_dwqhaarhpagex_none_po_kernel(
    tc, x_words, x_scales, d_words, d_scales, gs, mem, offs, ci, n1, n2, n3, k1, n4, out_0, out_1, out_2
):
    nc = tc.nc
    with ExitStack() as ctx:
        keep = ctx.enter_context(tc.tile_pool(name="keep", bufs=1))
        psum = ctx.enter_context(tc.psum_pool(name="psum", bufs=1))

        def load_list(src, name):
            tile = keep.tile(list(src.shape), U16, name=name)
            nc.sync.dma_start(tile[:], src)
            return tile

        def as_words(src):
            return src[0].rearrange("p n t -> p (n t)").bitcast(I32)

        x_rows = x_scales[0].bitcast(I32)
        d_rows = d_scales[0].bitcast(I32)
        mem_rows = mem.rearrange("(p t) c -> t p c", t=PACK)
        out_rows = out_0.rearrange("(p t) c -> t p c", t=PACK)

        d_table = keep.tile([P, G], U32)
        x_table = keep.tile([P, T], U32)
        d_bytes = keep.tile([P, G], U8)
        x_bytes = keep.tile([P, T], U8)
        d_run_bytes = keep.tile([P, G], U8)
        layer_scale = keep.tile([P, H], U8, align_bytes=64)
        nc.vector.memset(d_run_bytes[:].bitcast(I32), 0)
        nc.vector.memset(layer_scale[:].bitcast(I32), 0)

        ci_list = load_list(ci, "ci_list")
        for q in range(4):
            nc.sync.dma_start(
                d_bytes[32 * q : 32 * q + 32, :].bitcast(I32), d_rows[4 * q : 4 * q + 4, :].partition_broadcast(8)
            )
        nc.sync.dma_start(d_table[:].bitcast(I32), as_words(d_words))
        for q in range(4):
            nc.sync.dma_start(
                x_bytes[32 * q : 32 * q + 32, :].bitcast(I32), x_rows[4 * q : 4 * q + 4, :].partition_broadcast(8)
            )
        offs_list = load_list(offs, "offs_list")
        nc.sync.dma_start(x_table[:].bitcast(I32), as_words(x_words))
        gain = keep.tile([P, PACK], F32)
        nc.scalar.dma_start(gain[:], gs.rearrange("(p t) o -> p (t o)", t=PACK))
        n1_list = load_list(n1, "n1_list")
        n2_list = load_list(n2, "n2_list")
        k1_list = load_list(k1, "k1_list")
        for r in range(2):
            nc.sync.dma_start(d_run_bytes[r:P:16, :].bitcast(I32), d_rows[r:16:2, :])
        page = [keep.tile([P, U], F32, name="page%d" % t) for t in range(PACK)]
        n3_list = load_list(n3, "n3_list")
        n4_list = load_list(n4, "n4_list")
        for t in range(PACK):
            nc.sync.dma_start(page[t][:], mem_rows[t])

        gain16 = keep.tile([P, PACK], F32)
        nc.scalar.activation(gain16[:], gain[:], COPY, scale=0.0625)

        def dealt(ap):
            return ap.rearrange("p (t m) -> p m t", t=PACK)

        code_scale = keep.tile([P, H], U8, align_bytes=64)
        code_words = keep.tile([P, H], U32, align_bytes=64)
        tok_scale = keep.tile([P, S], U8, align_bytes=64)
        tok_words = keep.tile([P, S], U32, align_bytes=64)
        nc.vector.tensor_copy(dealt(code_scale[:]), d_bytes[:].indirect(ci_list[:]))
        nc.vector.tensor_copy(dealt(code_words[:]), d_table[:].indirect(ci_list[:]))
        nc.vector.tensor_copy(tok_scale[:], x_bytes[:].indirect(offs_list[:]))
        halves = [(slice(HALF * h, HALF * (h + 1)), slice(16 * h, 16 * (h + 1))) for h in range(2)]
        (cols_a, entries_a), (cols_b, entries_b) = halves
        every = slice(0, S)
        for cols, entries in halves:
            nc.vector.tensor_copy(tok_words[:, cols], x_table[:].indirect(offs_list[:, entries]))

        def product(acc, words, scale, t, moving_words, moving_scale, cols):
            rows = slice(P * t, P * (t + 1))
            nc.tensor.matmul_mx(
                out=acc,
                lhsT=words[:, rows].bitcast(FP8X4),
                lhsT_scale=scale[:, rows],
                rhs=moving_words[:, cols].bitcast(FP8X4),
                rhs_scale=moving_scale[:, cols],
                start=True,
                stop=True,
            )

        run_scale = keep.tile([P, H], U8)
        run_scale_dealt = keep.tile([P, H], U8)
        nc.vector.tensor_copy(run_scale[:], d_run_bytes[:].indirect(k1_list[:]))
        nc.vector.tensor_copy(dealt(run_scale_dealt[:]), run_scale[:].rearrange("p (m t) -> p m t", t=PACK))
        for r in range(4):
            first = 16 * (r // 2) + r % 2
            nc.sync.dma_start(layer_scale[r:P:32, :].bitcast(I32), run_scale_dealt[first:P:32, :].bitcast(I32))

        score, pa, pb, minus_pb, dt, partner, larger, held = {}, {}, {}, {}, {}, {}, {}, {}
        z_grouped = keep.tile([P, S, PACK], BF16, align_bytes=64)

        def leave_bank(t):
            score[t] = keep.tile([P, S], F32, name="score%d" % t)
            pieces = [(cols_a, 0), (cols_b, 1)] if t == 0 else [(every, (t + 1) % 2)]
            for cols, bank in pieces:
                acc = psum.tile([P, cols.stop - cols.start], F32, tag="score_bank%d" % bank)
                product(acc[:], code_words, code_scale, t, tok_words, tok_scale, cols)
                nc.scalar.activation(score[t][:, cols], acc[:], COPY)

        def fetch_pairs(t):
            pa[t] = keep.tile([P, W], F32, tag="pa%d" % t, name="pa%d" % t)
            pb[t] = keep.tile([P, W], F32, name="pb%d" % t)
            nc.scalar.activation(pa[t][:], score[t][:].indirect(n1_list[:]), COPY)
            nc.scalar.activation(pb[t][:], score[t][:].indirect(n2_list[:]), COPY)

        def put_sums(t):
            dt[t] = keep.tile([P, S], F32, tag="dt", bufs=2, name="dt%d" % t)
            nc.vector.tensor_tensor(dt[t][:].indirect(n1_list[:]), pa[t][:], pb[t][:], ADD)

        def put_differences(t):
            minus_pb[t] = keep.tile([P, W], F32, tag="late", align_bytes=64, name="minus_pb%d" % t)
            nc.scalar.activation(minus_pb[t][:], pb[t][:], COPY, scale=-1.0)
            nc.vector.tensor_tensor(dt[t][:].indirect(n2_list[:]), pa[t][:], minus_pb[t][:], ADD)

        def fetch_partners(t):
            partner[t] = keep.tile([P, S], F32, name="partner%d" % t)
            for cols, entries in halves:
                nc.scalar.activation(partner[t][:, cols], dt[t][:].indirect(n3_list[:, entries]), COPY)

        def take_larger(t, cols):
            if t not in larger:
                larger[t] = keep.tile([P, S], F32, tag="larger%d" % t, name="larger%d" % t)
            nc.vector.tensor_tensor(larger[t][:, cols], dt[t][:, cols], partner[t][:, cols], MAX)

        def weigh(t, cols):
            nc.scalar.activation(z_grouped[:, cols, t], larger[t][:, cols], COPY, scale=gain16[:, t : t + 1])

        def fetch_held(t):
            nc.scalar.activation(held[t], page[t][:].indirect(n4_list[:]), COPY, scale=0.5)

        leave_bank(0)
        fetch_pairs(0)
        put_sums(0)
        put_differences(0)
        leave_bank(1)
        fetch_pairs(1)
        put_sums(1)
        leave_bank(2)
        leave_bank(3)
        fetch_partners(0)
        take_larger(0, every)
        put_differences(1)
        fetch_pairs(2)
        put_sums(2)
        weigh(0, cols_a)
        fetch_partners(1)
        take_larger(1, every)
        put_differences(2)
        weigh(0, cols_b)
        fetch_pairs(3)
        put_sums(3)
        fetch_partners(2)
        take_larger(2, every)
        put_differences(3)
        weigh(1, every)
        z_last_two = keep.tile([P, 2, HALF], BF16)
        nc.scalar.activation(z_last_two[:, 0, :], larger[2][:, cols_a], COPY, scale=gain16[:, 2:3])
        weigh(2, cols_b)

        run_words = keep.tile([P, H], U32, tag="late", align_bytes=64)
        layer_words = keep.tile([P, H], U32, align_bytes=64)
        nc.vector.tensor_copy(run_words[:], d_table[:].indirect(k1_list[:]))
        nc.vector.tensor_copy(
            dealt(layer_words[:].bitcast(I32)), run_words[:].bitcast(I32).rearrange("p (m t) -> p m t", t=PACK)
        )

        fetch_partners(3)
        held_first = keep.tile([P, S], F32, tag="pa3")
        held[0] = held_first[:]
        fetch_held(0)
        z_words = keep.tile([P, S], U32, align_bytes=64)
        z_scale = keep.tile([P, S], U8, align_bytes=64)
        take_larger(3, cols_a)
        take_larger(3, cols_b)
        nc.vector.tensor_scalar(z_last_two[:, 1, :], larger[3][:, cols_a], gain16[:, 3:4], None, MULT)
        nc.vector.tensor_copy(z_grouped[:, cols_a, 2:4], z_last_two[:].rearrange("p t c -> p c t"))
        weigh(3, cols_b)
        first_acc = [psum.tile([P, HALF], F32, name="first_acc%d" % h) for h in range(2)]
        later_acc = [psum.tile([P, S], F32, name="later_acc%d" % t) for t in range(1, PACK)]
        for h, (cols, entries) in enumerate(halves):
            nc.vector.quantize_mx(
                out=z_words[:, cols].bitcast(FP8X4),
                scales=z_scale[:, cols],
                in_=z_grouped[:, cols, :].rearrange("p c t -> p (c t)"),
            )
            for t in range(PACK):
                acc = first_acc[h][:] if t == 0 else later_acc[t - 1][:, cols]
                product(acc, layer_words, layer_scale, t, z_words, z_scale, cols)
        held_rest = keep.tile([P, PACK - 1, S], F32, tag="larger3")
        for t in range(1, PACK):
            held[t] = held_rest[:, t - 1, :]
            fetch_held(t)

        low = keep.tile([P, U // 2, PACK], BF16, align_bytes=64)
        high = keep.tile([P, U // 2, PACK], BF16, align_bytes=64)
        last_two = keep.tile([P, 2, U // 2], BF16)
        fresh = keep.tile([P, 2, S], F32)

        def renew(t, acc, cols):
            nc.vector.scalar_tensor_tensor(fresh[:, t % 2, cols], acc, 0.0625, held[t][:, cols], MULT, MAX)

        def put_back(t, cols, entries):
            nc.vector.tensor_copy(page[t][:].indirect(n4_list[:, entries]), fresh[:, t % 2, cols])

        def hand_out(t):
            nc.sync.dma_start(out_rows[t], page[t][:])
            if t < 2:
                nc.scalar.activation(low[:, :, t], page[t][:, : U // 2], COPY)
            elif t == 2:
                nc.scalar.activation(last_two[:, 0, :], page[t][:, : U // 2], COPY)
            if t < 3:
                nc.scalar.activation(high[:, :, t], page[t][:, U // 2 :], COPY)

        all_entries = slice(0, S // 16)
        renew(0, first_acc[0][:], cols_a)
        put_back(0, cols_a, entries_a)
        renew(0, first_acc[1][:], cols_b)
        renew(1, later_acc[0][:], every)
        put_back(0, cols_b, entries_b)
        hand_out(0)
        for t in range(1, PACK):
            put_back(t, every, all_entries)
            hand_out(t)
            if t + 1 < PACK:
                renew(t + 1, later_acc[t][:], every)

        out_words = keep.tile([P, U], U32, align_bytes=64)
        out_scale = keep.tile([P, U], U8, align_bytes=64)

        def quantise_quarter(grouped, first, place):
            cols = slice(place, place + QUARTER)
            nc.vector.quantize_mx(
                out=out_words[:, cols].bitcast(FP8X4),
                scales=out_scale[:, cols],
                in_=grouped[:, first : first + QUARTER, :].rearrange("p c t -> p (c t)"),
            )

        for first in (0, QUARTER):
            nc.scalar.activation(
                high[:, first : first + QUARTER, 3], page[3][:, U // 2 + first : U // 2 + first + QUARTER], COPY
            )
        nc.vector.tensor_copy(last_two[:, 1, :], page[3][:, : U // 2])
        for first in (0, QUARTER):
            nc.vector.tensor_copy(
                low[:, first : first + QUARTER, 2:4],
                last_two[:, :, first : first + QUARTER].rearrange("p t c -> p c t"),
            )
        quantise_quarter(high, 0, U // 2)
        quantise_quarter(low, 0, 0)
        quantise_quarter(low, QUARTER, QUARTER)
        words_out = as_words(out_1)
        nc.sync.dma_start(words_out[:, : U // 2], out_words[:, : U // 2].bitcast(I32))
        quantise_quarter(high, QUARTER, U // 2 + QUARTER)
        nc.sync.dma_start(words_out[:, U // 2 :], out_words[:, U // 2 :].bitcast(I32))
        scale_out = out_2[0].bitcast(I32)
        for q in range(4):
            queue = nc.scalar if q % 2 == 0 else nc.sync
            queue.dma_start(scale_out[4 * q : 4 * q + 4, :], out_scale[32 * q : 32 * q + 4, :].bitcast(I32))
